import numpy as np
import ml_dtypes


def mxq(x, axis, fmt="e4m3"):
    dtype, down = {"e4m3": (ml_dtypes.float8_e4m3fn, 7), "e5m2": (ml_dtypes.float8_e5m2, 14)}[fmt]
    v = np.moveaxis(np.asarray(x, np.float32).astype(ml_dtypes.bfloat16).astype(np.float64), axis, -1)
    blocks = v.reshape(v.shape[:-1] + (-1, 32))
    amax = np.abs(blocks).max(-1, keepdims=True)
    byte = np.maximum(np.where(amax > 0, np.frexp(amax)[1] - 1 + 127, 0) - down, 1)
    scale = np.exp2(byte - 127.0)
    codes = (blocks / scale).astype(np.float32).astype(dtype).astype(np.float64)
    return np.moveaxis((codes * scale).reshape(v.shape), -1, axis)


WIDE = False


def mx_kscale(k):
    if not WIDE:
        return np.ones(k)
    levels = np.array([10, -10, 5, -5, 0])
    if k % 512:
        return np.exp2(np.random.permutation(np.resize(levels, k // 32))).repeat(32)
    a = np.empty((k // 512, 16))
    for p in range(k // 512):
        a[p, :8] = np.random.permutation(np.resize(levels, 8))
        for g in range(8):
            far = levels[np.abs(levels - a[p, g]) >= 10]
            a[p, g + 8] = far[np.random.randint(len(far))]
    return np.exp2(a.ravel()).repeat(32)


BF16 = ml_dtypes.bfloat16


def bf(x):
    return np.asarray(x, np.float32).astype(BF16)


def f64(x):
    return np.asarray(x).astype(np.float64)


D, C, L = 1536, 1024, 512


def setup_inputs():
    s, t, u = mx_kscale(D), mx_kscale(C), mx_kscale(D)
    m = np.abs(np.random.standard_normal((L, D)))
    m = m / np.sqrt((m * m).sum(axis=1, keepdims=True))
    return {"logs": bf(np.random.standard_normal((D, C)) * s[:, None] * t),
            "depth_filter": bf(np.random.standard_normal((D, D)) / (3 * np.sqrt(D)) * s[:, None] / s),
            "tool_correction": bf(np.random.standard_normal((C, C)) / (3 * np.sqrt(C)) / t[:, None] * t),
            "porosity_gate": bf(np.random.uniform(0.25, 1.0, D) * u / s),
            "group_weights": bf(m / u),
            "channel_gain": bf((1 + 0.1 * np.random.standard_normal(C)) / t)}


def reference(logs, depth_filter, tool_correction, porosity_gate, group_weights, channel_gain):
    x = f64(logs)
    y = x + (mxq(f64(depth_filter), 1, "e4m3") @ mxq(x, 0, "e4m3"))
    z = y + (mxq(y, 1, "e4m3") @ mxq(f64(tool_correction), 0, "e4m3"))
    v = z * f64(porosity_gate)[:, None]
    stack = mxq(f64(group_weights), 1, "e4m3") @ mxq(v, 0, "e4m3")
    return stack * f64(channel_gain)

from contextlib import ExitStack

import concourse.mybir as mybir
from concourse.masks import make_identity

D, C, L = 1536, 1024, 512
FLOPS = 2 * D * D * C + 2 * D * C * C + 2 * L * D * C

F32 = mybir.dt.float32
BF16 = mybir.dt.bfloat16
U32 = mybir.dt.uint32
U8 = mybir.dt.uint8
FP8X4 = mybir.dt.float8_e4m3fn_x4
COPY = mybir.ActivationFunctionType.Copy
MULT = mybir.AluOpType.mult
ADD = mybir.AluOpType.add

P = 128
PACK = 4
HALF = 512
KD = D // 512
KC = C // 512
TILES = D // P
ROWS_OUT = L // P


def tile_well_log_group_stack_t1_kernel(
    tc, logs, depth_filter, tool_correction, porosity_gate, group_weights, channel_gain, out
):
    nc = tc.nc
    with ExitStack() as ctx:
        keep = ctx.enter_context(tc.tile_pool(name="keep", bufs=1))
        work = ctx.enter_context(tc.tile_pool(name="work", bufs=3))
        turn = ctx.enter_context(tc.psum_pool(name="turn", bufs=3))
        sums = ctx.enter_context(tc.psum_pool(name="sums", bufs=5))

        x_raw, x_codes, x_scales = {}, {}, {}
        t_raw, t_codes, t_scales = {}, {}, {}
        row_raw, row_bank, row_pairs, row_codes = {}, {}, {}, {}
        acc1, acc2, acc3 = {}, {}, {}
        y32, y16, y_gated, y_bank, y_pairs, y_codes = {}, {}, {}, {}, {}, {}
        v16, v_grouped, v_codes, v_scales = {}, {}, {}, {}

        def copy(engine, dst, src):
            if engine == "S":
                nc.scalar.copy(out=dst, in_=src)
            else:
                nc.vector.tensor_copy(out=dst, in_=src)

        def load_x(g, n):
            t = keep.tile([P, PACK, HALF], BF16, name="x_raw%d%d" % (g, n), align_bytes=64)
            x_raw[g, n] = t
            rows = logs[512 * g : 512 * (g + 1), HALF * n : HALF * (n + 1)]
            nc.sync.dma_start(out=t[:], in_=rows.rearrange("(p j) w -> p j w", j=PACK))

        def load_t(h):
            t = keep.tile([P, PACK, C], BF16, name="t_raw%d" % h, align_bytes=64)
            t_raw[h] = t
            rows = tool_correction[512 * h : 512 * (h + 1), :]
            nc.sync.dma_start(out=t[:], in_=rows.rearrange("(p j) w -> p j w", j=PACK))

        def load_rows(i):
            t = work.tile([P, D], BF16, name="row_raw", bufs=8, align_bytes=64)
            row_raw[i] = t
            if i < TILES:
                src = depth_filter.rearrange("(g m t) k -> g t m k", m=P, t=PACK)[i // PACK, i % PACK]
            else:
                m = i - TILES
                src = group_weights[P * m : P * (m + 1), :]
            nc.sync.dma_start(out=t[:], in_=src)

        def group_cols(engine, dst, src, c0, c1):
            copy(
                engine,
                dst[:, c0:c1, :].rearrange("p (c i) t -> p c t i", i=4),
                src[:, :, c0:c1].rearrange("p t (c i) -> p c t i", i=4),
            )

        def x_group(g, n, engine, c0=0, c1=HALF):
            if (g, n) not in x_codes:
                x_codes[g, n] = work.tile([P, HALF, PACK], BF16, name="grouped", bufs=3, align_bytes=64)
            group_cols(engine, x_codes[g, n], x_raw[g, n], c0, c1)

        def quant(dst, name, grouped, cols):
            codes = keep.tile([P, cols], U32, name=name + "c", align_bytes=64)
            scales = keep.tile([P, cols], U8, name=name + "s", align_bytes=64)
            nc.vector.quantize_mx(
                out=codes[:].bitcast(FP8X4), scales=scales[:], in_=grouped[:].rearrange("p c t -> p (c t)")
            )
            return codes, scales

        def x_quant(g, n):
            x_codes[g, n] = quant(x_codes, "x%d%d" % (g, n), x_codes[g, n], HALF)

        def t_group(h, n, engine, c0=0, c1=HALF):
            if (h, n) not in t_codes:
                t_codes[h, n] = work.tile([P, HALF, PACK], BF16, name="grouped", bufs=3, align_bytes=64)
            group_cols(engine, t_codes[h, n], t_raw[h][:, :, HALF * n : HALF * (n + 1)], c0, c1)

        def t_quant(h, n):
            t_codes[h, n] = quant(t_codes, "t%d%d" % (h, n), t_codes[h, n], HALF)

        def row_turn(j):
            first = turn.tile([P, 2, 2, P], F32, name="bank")
            both = turn.tile([P, 2, 2, P], F32, name="bank")
            second = turn.tile([P, 2, 2, P], F32, name="bank")

            def one(i, h, dst):
                words = row_raw[i][:].bitcast(F32)
                for u in range(2):
                    nc.tensor.transpose(dst[:, u, :], words[:, 256 * h + u : 256 * (h + 1) : 2], ident[:])

            one(2 * j, 0, first[:, 0])
            one(2 * j, 1, first[:, 1])
            one(2 * j, 2, both[:, 0])
            one(2 * j + 1, 2, both[:, 1])
            one(2 * j + 1, 0, second[:, 0])
            one(2 * j + 1, 1, second[:, 1])
            row_bank[j] = (first, both, second)

        def row_copy(j, part, engine="S"):
            t = work.tile([P, 2, P, 2], F32, name="row_pairs", bufs=4, align_bytes=64)
            row_pairs[j, part] = t
            copy(engine, t[:], row_bank[j][part][:].rearrange("p h u m -> p h m u"))

        def row_quant(j, part):
            pool_tag = "rs" if j < TILES // 2 else "rg"
            bufs = 9 if j < TILES // 2 else 6
            codes = work.tile([P, 2, P], U32, name="%sc" % pool_tag, bufs=bufs, align_bytes=64)
            scales = work.tile([P, 2, P], U8, name="%ss" % pool_tag, bufs=bufs, align_bytes=64)
            nc.vector.quantize_mx(
                out=codes[:].rearrange("p h m -> p (h m)").bitcast(FP8X4),
                scales=scales[:].rearrange("p h m -> p (h m)"),
                in_=row_pairs[j, part][:].rearrange("p h m u -> p (h m u)").bitcast(BF16),
            )
            for q in range(2):
                i, h = ((2 * j, q), (2 * j + q, 2), (2 * j + 1, q))[part]
                row_codes[i, h] = (codes[:, q, :], scales[:, q, :])

        def mx(acc, lhs, rhs, n0, start, stop):
            nc.tensor.matmul_mx(
                out=acc,
                lhsT=lhs[0].bitcast(FP8X4),
                lhsT_scale=lhs[1],
                rhs=rhs[0][:, n0 : n0 + HALF].bitcast(FP8X4),
                rhs_scale=rhs[1][:, n0 : n0 + HALF],
                start=start,
                stop=stop,
            )

        def stage1(i, n):
            acc = sums.tile([P, HALF], F32, name="acc")
            for h in range(KD):
                mx(acc[:], row_codes[i, h], x_codes[h, n], 0, h == 0, h == KD - 1)
            acc1[i, n] = acc

        def y_add(i, n):
            t = work.tile([P, HALF], F32, name="y32", bufs=4, align_bytes=64)
            y32[i, n] = t
            nc.vector.tensor_tensor(
                out=t[:], in0=acc1[i, n][:], in1=x_raw[i // PACK, n][:, i % PACK, :], op=ADD
            )

        def y_cast(i, n, engine="S"):
            t = work.tile([P, 2, P, 2], BF16, name="y16", bufs=12, align_bytes=64)
            y16[i, n] = t
            copy(engine, t[:], y32[i, n][:].rearrange("p (q u e) -> p u q e", u=2, e=2))

        def y_gate(i, n, engine="S"):
            t = work.tile([P, HALF], F32, name="y_gated", bufs=16, align_bytes=64)
            y_gated[i, n] = t
            if engine == "S":
                nc.scalar.activation(out=t[:], in_=y32[i, n][:], func=COPY, scale=gate[:, i : i + 1])
            elif engine == "G":
                nc.gpsimd.tensor_scalar(
                    out=t[:], in0=y32[i, n][:], scalar1=gate[:, i : i + 1], scalar2=0.0, op0=MULT, op1=ADD
                )
            else:
                nc.vector.tensor_scalar(
                    out=t[:], in0=y32[i, n][:], scalar1=gate[:, i : i + 1], scalar2=None, op0=MULT
                )

        def y_turn(i):
            bank = turn.tile([P, 2, 2, P], F32, name="bank")
            for h in range(KC):
                words = y16[i, h][:].rearrange("p u q e -> p (u q e)").bitcast(F32)
                for u in range(2):
                    nc.tensor.transpose(bank[:, h, u, :], words[:, P * u : P * (u + 1)], ident[:])
            y_bank[i] = bank

        def y_copy(i, engine="S"):
            t = work.tile([P, 2, P, 2], F32, name="y_pairs", bufs=2, align_bytes=64)
            y_pairs[i] = t
            copy(engine, t[:], y_bank[i][:].rearrange("p h u m -> p h m u"))

        def y_quant(i):
            codes = work.tile([P, 2, P], U32, name="y_codes", bufs=5, align_bytes=64)
            scales = work.tile([P, 2, P], U8, name="y_scales", bufs=5, align_bytes=64)
            nc.vector.quantize_mx(
                out=codes[:].rearrange("p h m -> p (h m)").bitcast(FP8X4),
                scales=scales[:].rearrange("p h m -> p (h m)"),
                in_=y_pairs[i][:].rearrange("p h m u -> p (h m u)").bitcast(BF16),
            )
            y_codes[i] = (codes, scales)

        def stage2(i, n):
            acc = sums.tile([P, HALF], F32, name="acc")
            codes, scales = y_codes[i]
            for h in range(KC):
                mx(acc[:], (codes[:, h, :], scales[:, h, :]), t_codes[h, n], 0, h == 0, h == KC - 1)
            acc2[i, n] = acc

        def v_add(i, n):
            g, t = i // PACK, i % PACK
            if t == 0:
                v16[g, n] = work.tile([P, PACK, HALF], BF16, name="v16", bufs=4, align_bytes=64)
            nc.vector.scalar_tensor_tensor(
                out=v16[g, n][:, t, :],
                in0=acc2[i, n][:],
                scalar=gate[:, i : i + 1],
                in1=y_gated[i, n][:],
                op0=MULT,
                op1=ADD,
            )

        def v_group(g, n, engine, c0=0, c1=HALF):
            if (g, n) not in v_codes:
                v_codes[g, n] = work.tile([P, HALF, PACK], BF16, name="grouped", bufs=3, align_bytes=64)
            group_cols(engine, v_codes[g, n], v16[g, n], c0, c1)

        def v_quant(g, n):
            v_codes[g, n] = quant(v_codes, "v%d%d" % (g, n), v_codes[g, n], HALF)

        def stage3(m, n, h, pool=None):
            if h == 0:
                pool = pool or sums
                acc3[m, n] = pool.tile([P, HALF], F32, name="acc" if pool is sums else "bank")
            mx(acc3[m, n][:], row_codes[TILES + m, h], v_codes[h, n], 0, h == 0, h == KD - 1)

        def finish(m, n, engine="V"):
            t = work.tile([P, HALF], F32, name="y_gated", bufs=16, align_bytes=64)
            gain_cols = gain[:, HALF * n : HALF * (n + 1)]
            if engine == "V":
                nc.vector.tensor_tensor(out=t[:], in0=acc3[m, n][:], in1=gain_cols, op=MULT)
            else:
                raw = work.tile([P, HALF], F32, name="result_raw", bufs=2, align_bytes=64)
                nc.scalar.copy(out=raw[:], in_=acc3[m, n][:])
                nc.gpsimd.tensor_tensor(out=t[:], in0=raw[:], in1=gain_cols, op=MULT)
            nc.sync.dma_start(out=out[P * m : P * (m + 1), HALF * n : HALF * (n + 1)], in_=t[:])

        ident = keep.tile([P, P], F32, name="ident", align_bytes=64)
        make_identity(nc, ident[:])
        gate16 = keep.tile([P, TILES], BF16, name="gate16", align_bytes=64)
        gate = keep.tile([P, TILES], F32, name="gate", align_bytes=64)
        gain = keep.tile([P, C], BF16, name="gain", align_bytes=64)
        warm = keep.tile([P, 1], F32, name="warm", align_bytes=64)
        nc.vector.memset(warm[:], 0.0)
        nc.scalar.activation(out=warm[:], in_=warm[:], func=COPY)

        for g in range(KD):
            load_x(g, 0)
        load_rows(0)
        load_rows(1)
        load_rows(2)
        load_rows(3)
        nc.sync.dma_start(
            out=gate16[:].rearrange("p (g t) -> p g t", t=PACK),
            in_=porosity_gate.rearrange("(g p t) -> p g t", p=P, t=PACK),
        )
        for g in range(KD):
            load_x(g, 1)
        load_t(0)
        load_t(1)
        load_rows(4)
        load_rows(5)
        load_rows(6)
        load_rows(7)

        XS = 352
        def x_half(n):
            x_group(0, n, "V", 0, XS)
            x_group(0, n, "S", XS, HALF)
            x_group(1, n, "V", 0, XS)
            x_group(1, n, "S", XS, HALF)
            x_quant(0, n)
            x_group(2, n, "V", 0, XS)
            x_group(2, n, "S", XS, HALF)
            x_quant(1, n)
        def rows(j, e):
            for p in range(3):
                row_copy(j, p, e[p])
        def rowq(j):
            for p in range(3):
                row_quant(j, p)
        def ya(i, n):
            y_add(i, n)
            y_cast(i, n)
        def yg(i, n):
            y_gate(i, n, GATE[(i + n) % len(GATE)])

        x_half(0)
        row_turn(0)
        rows(0, "SSS")
        row_quant(0, 0)
        x_quant(2, 0)
        row_quant(0, 1)
        row_quant(0, 2)
        nc.vector.tensor_copy(out=gate[:], in_=gate16[:])
        stage1(0, 0)
        stage1(1, 0)
        row_turn(1)
        rows(1, "SSS")
        x_half(1)
        rowq(1)
        x_quant(2, 1)
        stage1(2, 0)
        stage1(3, 0)
        for i in range(4):
            ya(i, 0)
        row_turn(2)
        rows(2, "SSS")
        for i in range(4):
            stage1(i, 1)
        rowq(2)
        t_group(0, 0, "V", 0, XS)
        t_group(0, 0, "S", XS, HALF)
        for i in range(4):
            ya(i, 1)
            yg(i, 0)
            yg(i, 1)
        t_quant(0, 0)

        def step(s):
            for f in EXTRA_V0.get(s, []):
                run(f)
            if s + 3 < 8:
                row_turn(s + 3)
                rows(s + 3, "SSS")
                for k in (0, 1):
                    if s + 5 < 8 :
                        load_rows(2 * (s + 4) + k)
                    elif s + 4 < 8:
                        load_rows(2 * (s + 4) + k)
            if s < 6:
                for i in (2 * s, 2 * s + 1):
                    y_turn(i)
                for i in (2 * s, 2 * s + 1):
                    y_copy(i, YP)
                    y_quant(i)
            if s + 3 < 8:
                rowq(s + 3)
            if s + 2 < 6:
                for i in (2 * s + 4, 2 * s + 5):
                    for n in range(2):
                        stage1(i, n)
                        ya(i, n)
                        yg(i, n)
            for f in EXTRA_S.get(s, []):
                run(f)
            if s >= 1:
                for n in range(2):
                    for i in (2 * s - 2, 2 * s - 1):
                        stage2(i, n)
                        v_add(i, n)
            for f in EXTRA_V1.get(s, []):
                run(f)

        def run(f):
            dict(t=t_group, tq=t_quant, v=v_group, vq=v_quant, C=cpass)[f[0]](*f[1:])

        def cpass(h, ns=(0, 1)):
            for n in ns:
                for m in range(4):
                    stage3(m, n, h, turn if POOLC[n * 4 + m] == "t" else sums)

        for s in range(7):
            step(s)
            if s == 1:
                nc.sync.dma_start(out=gain[:], in_=channel_gain.partition_broadcast(P))
        VS = 192
        v_group(2, 0, "V", 0, VS)
        v_group(2, 0, "S", VS, 512)
        v_group(2, 1, "V", 0, VS)
        v_group(2, 1, "S", VS, 512)
        v_quant(2, 0)
        v_quant(2, 1)
        for n in range(2):
            for h in range(2):
                cpass(h, (n,))
            for m in range(4):
                stage3(m, n, 2)
                finish(m, n, FIN[n * 4 + m])


GATE = "G"
YP = "S"
FIN = "VVVVSVVV"
XV = 352
EXTRA_V0 = {0: [("t", 1, 0, "V",0,256),("t", 1, 0, "S",256,512), ("t", 0, 1, "V", 0, 256), ("tq", 1, 0)],
}
EXTRA_S = {0: [("t", 0, 1, "S", 256, 512), ("t", 1, 1, "S"), ("tq", 0, 1), ("tq",1,1)],
   3: [("v", 0, 0, "S"), ("v",0,1,"S")],
   5: [("v", 1, 0, "S"), ("v",1,1,"S")],
}
EXTRA_V1 = {3: [("vq", 0, 0),("vq",0,1)], 5:[("vq", 1, 0),("vq",1,1)] }
POOLC = "sssssttt"
